import numpy as np
import ml_dtypes


def mxq(x, axis, fmt="e4m3"):
    dtype, down = {"e4m3": (ml_dtypes.float8_e4m3fn, 7), "e5m2": (ml_dtypes.float8_e5m2, 14)}[fmt]
    v = np.moveaxis(np.asarray(x, np.float32).astype(ml_dtypes.bfloat16).astype(np.float64), axis, -1)
    blocks = v.reshape(v.shape[:-1] + (-1, 32))
    amax = np.abs(blocks).max(-1, keepdims=True)
    byte = np.maximum(np.where(amax > 0, np.frexp(amax)[1] - 1 + 127, 0) - down, 1)
    scale = np.exp2(byte - 127.0)
    codes = (blocks / scale).astype(np.float32).astype(dtype).astype(np.float64)
    return np.moveaxis((codes * scale).reshape(v.shape), -1, axis)


WIDE = False


def mx_kscale(k, group=512):
    if not WIDE:
        return np.ones(k)
    levels = np.array([10, -10, 5, -5, 0])
    if group != 512:
        return np.exp2(np.random.permutation(np.resize(levels, k // group))).repeat(group)
    if k % 512:
        return np.exp2(np.random.permutation(np.resize(levels, k // 32))).repeat(32)
    a = np.empty((k // 512, 16))
    for p in range(k // 512):
        a[p, :8] = np.random.permutation(np.resize(levels, 8))
        for g in range(8):
            far = levels[np.abs(levels - a[p, g]) >= 10]
            a[p, g + 8] = far[np.random.randint(len(far))]
    return np.exp2(a.ravel()).repeat(32)


def f64(x):
    return np.asarray(x).astype(np.float64)


def striped(idx):
    return np.tile(np.asarray(idx).reshape(-1, 16).T, (8, 1)).astype(np.uint16)


def unstriped(offs):
    return offs[:16].T.reshape(-1).astype(np.int64)


H, KV, D, NQ, N = 4, 4, 256, 512, 512


def setup_inputs():
    n = np.random.standard_normal
    s = mx_kscale(D, 0)[:, None]
    u = mx_kscale(N)
    t = np.random.uniform(0.5, 2.0, N) * u
    v = n((KV, N, 128))
    v[:, :, 127] = 1.0
    return {
        "qT": (n((H, D, NQ)) * s * (0.70 / np.sqrt(D))).astype(np.float32),
        "kT": (n((KV, D, N)) / s).astype(np.float32),
        "t": t.reshape(N, 1).astype(np.float32),
        "v": (v / t[:, None]).astype(np.float32),
        "og": n((H, NQ, 128)).astype(np.float32),
    }


def reference(qT, kT, t, v, og):
    a = mxq(f64(kT), 1, "e4m3").transpose(0, 2, 1) @ mxq(f64(qT), 1, "e4m3")
    p = np.square(np.maximum(a, 0.0))
    w = p * f64(t)
    y = mxq(w, 1, "e4m3").transpose(0, 2, 1) @ mxq(f64(v), 1, "e4m3")
    y = y / (y[:, :, 127:128] + 1.0)
    y = y / (1.0 + np.exp(-f64(og)))
    return y

@@ -1,0 +1,268 @@
+from contextlib import ExitStack
+
+import concourse.mybir as mybir
+
+H, D, NQ, N, E = 4, 256, 512, 512, 128
+FLOPS = 2 * H * N * NQ * D + 2 * H * NQ * N * E
+
+F32 = mybir.dt.float32
+BF16 = mybir.dt.bfloat16
+U32 = mybir.dt.uint32
+U8 = mybir.dt.uint8
+FP8X4 = mybir.dt.float8_e4m3fn_x4
+ACT = mybir.ActivationFunctionType
+ALU = mybir.AluOpType
+
+P = 128
+PACK = 4
+ROWS = 64
+PAIRS = 2
+HALF = 256
+UNITS = 16
+BANKS = 3
+
+
+def tile_rows_a_relu2_gate_kernel(tc, qT, kT, t, v, og, out):
+    nc = tc.nc
+    with ExitStack() as ctx:
+        sb = ctx.enter_context(tc.tile_pool(name="sb", bufs=1))
+        ps = ctx.enter_context(tc.psum_pool(name="ps", bufs=1))
+        ctx.enter_context(tc.manual_schedule())
+
+        def tiles(name, count, shape, dtype, pool=sb):
+            if pool is sb:
+                return [pool.tile(shape, dtype, name=name + str(i), align_bytes=64) for i in range(count)]
+            return [pool.tile(shape, dtype, name=name + str(i)) for i in range(count)]
+
+        k_raw = tiles("k_raw", 2, [P, PACK, N], F32)
+        q_raw = tiles("q_raw", 4, [P, PACK, HALF], F32)
+        v_raw = tiles("v_raw", 2, [P, 2, PACK, E], F32)
+        og_raw = tiles("og_raw", 2, [P, 4, 2 * E], F32)
+        gate = tiles("gate", 2, [P, 4, 2 * E], F32)
+        k_bf = tiles("k_bf", 2, [P, PACK, P, PACK], BF16)
+        q_bf = tiles("q_bf", 4, [P, 2, P, PACK], BF16)
+        v_bf = tiles("v_bf", 2, [P, 2, E, PACK], BF16)
+        k_codes = tiles("k_codes", 2, [P, N], U32)
+        k_scales = tiles("k_scales", 2, [P, N], U8)
+        q_codes = tiles("q_codes", 4, [P, HALF], U32)
+        q_scales = tiles("q_scales", 4, [P, HALF], U8)
+        v_codes = tiles("v_codes", 2, [P, 2 * E], U32)
+        v_scales = tiles("v_scales", 2, [P, 2 * E], U8)
+        ta = tiles("ta", UNITS, [P, PACK, P], F32)
+        w_bf = tiles("w_bf", UNITS, [P, P, PACK], BF16)
+        w_codes = tiles("w_codes", UNITS, [P, P], U32)
+        w_scales = tiles("w_scales", UNITS, [P, P], U8)
+        den = tiles("den", 8, [P, 2], F32)
+        inv = tiles("inv", 8, [P, 2], F32)
+        res = tiles("res", 8, [P, 2, E], F32)
+        t_sb = sb.tile([P, PACK], F32, name="t_sb", align_bytes=64)
+        warm_in = sb.tile([P, 1], F32, name="warm_in", align_bytes=64)
+        warm_out = sb.tile([P, 1], F32, name="warm_out", align_bytes=64)
+        score = tiles("score", 2 * BANKS, [P, PACK, P], F32, ps)
+        acc = tiles("acc", 2, [P, 4, E], F32, ps)
+
+        def load_k(g):
+            nc.sync.dma_start(out=k_raw[g][:], in_=kT[2 * g : 2 * g + 2].rearrange("h (p j) n -> (h p) j n", j=PACK))
+
+        def load_q(g, c):
+            rows = qT[2 * g : 2 * g + 2].rearrange("h (p j) n -> (h p) j n", j=PACK)
+            nc.sync.dma_start(out=q_raw[2 * g + c][:], in_=rows[:, :, c * HALF : (c + 1) * HALF])
+
+        def load_v(g):
+            nc.sync.dma_start(
+                out=v_raw[g][:].rearrange("p h j e -> p h (j e)"),
+                in_=v[2 * g : 2 * g + 2].rearrange("h (p j) e -> p h (j e)", j=PACK),
+            )
+
+        def load_og(g):
+            nc.sync.dma_start(
+                out=og_raw[g][:],
+                in_=og[2 * g : 2 * g + 2].rearrange("h (c p x) e -> p (h c) (x e)", c=2, x=2),
+            )
+
+        def copy(engine, dst, src):
+            if engine == "v":
+                nc.vector.tensor_copy(out=dst, in_=src)
+            else:
+                nc.scalar.copy(out=dst, in_=src)
+
+        def deal_k(engine, g, s0, s1):
+            dst = k_bf[g][:].rearrange("p r s j -> p s j r")
+            src = k_raw[g][:].rearrange("p j (s r) -> p s j r", r=PACK)
+            copy(engine, dst[:, s0:s1], src[:, s0:s1])
+
+        def deal_q(engine, i, s0, s1):
+            dst = q_bf[i][:].rearrange("p x s j -> p s j x")
+            src = q_raw[i][:].rearrange("p j (s x) -> p s j x", x=2)
+            copy(engine, dst[:, s0:s1], src[:, s0:s1])
+
+        def deal_v(engine, g, h):
+            dst = v_bf[g][:, h].rearrange("p (c i) j -> p c j i", i=4)
+            src = v_raw[g][:, h].rearrange("p j (c i) -> p c j i", i=4)
+            copy(engine, dst, src)
+
+        def quant(codes, scales, src):
+            nc.vector.quantize_mx(out=codes[:].bitcast(FP8X4), scales=scales[:], in_=src)
+
+        def quant_k(g):
+            quant(k_codes[g], k_scales[g], k_bf[g][:].rearrange("p r s j -> p (r s j)"))
+
+        def quant_q(i):
+            quant(q_codes[i], q_scales[i], q_bf[i][:].rearrange("p x s j -> p (x s j)"))
+
+        def quant_v(g):
+            quant(v_codes[g], v_scales[g], v_bf[g][:].rearrange("p h e j -> p (h e j)"))
+
+        def quant_w(n):
+            quant(w_codes[n], w_scales[n], w_bf[n][:].rearrange("p s j -> p (s j)"))
+
+        def parts(n):
+            return n // 8, (n // 4) % 2, (n // 2) % 2, n % 2
+
+        def bank(n):
+            return score[(n % 2) * BANKS + (n // 2) % BANKS]
+
+        def scores(n):
+            g, c, x, h = parts(n)
+            rows = slice(h * ROWS, (h + 1) * ROWS)
+            cols = slice(x * P, (x + 1) * P)
+            for r in range(PACK):
+                keys = slice(r * P, (r + 1) * P)
+                nc.tensor.matmul_mx(
+                    out=bank(n)[:, r, :],
+                    lhsT=k_codes[g][rows, keys].bitcast(FP8X4),
+                    lhsT_scale=k_scales[g][rows, keys],
+                    rhs=q_codes[2 * g + c][rows, cols].bitcast(FP8X4),
+                    rhs_scale=q_scales[2 * g + c][rows, cols],
+                    start=True,
+                    stop=True,
+                )
+
+        def scale(n):
+            for r in range(PACK):
+                nc.scalar.activation(out=ta[n][:, r, :], in_=bank(n)[:, r, :], func=ACT.Copy, scale=t_sb[:, r : r + 1])
+
+        def weigh(n):
+            nc.vector.scalar_tensor_tensor(
+                out=w_bf[n][:],
+                in0=bank(n)[:].rearrange("p r s -> p s r"),
+                scalar=0.0,
+                in1=ta[n][:].rearrange("p r s -> p s r"),
+                op0=ALU.max,
+                op1=ALU.mult,
+            )
+
+        def mix(n):
+            g, c, x, h = parts(n)
+            cols = slice(h * E, (h + 1) * E)
+            nc.tensor.matmul_mx(
+                out=acc[h][:, 2 * c + x, :],
+                lhsT=w_codes[n][:].bitcast(FP8X4),
+                lhsT_scale=w_scales[n][:],
+                rhs=v_codes[g][:, cols].bitcast(FP8X4),
+                rhs_scale=v_scales[g][:, cols],
+                start=True,
+                stop=True,
+            )
+
+        def sigmoid(g, h):
+            nc.scalar.activation(out=gate[g][:, 2 * h : 2 * h + 2, :], in_=og_raw[g][:, 2 * h : 2 * h + 2, :], func=ACT.Sigmoid)
+
+        def denom(g, c, h):
+            i = 4 * g + 2 * c + h
+            nc.vector.tensor_scalar_add(out=den[i][:], in0=acc[h][:, 2 * c : 2 * c + 2, E - 1], scalar1=1.0)
+
+        def invert(g, c, h):
+            i = 4 * g + 2 * c + h
+            nc.vector.reciprocal(out=inv[i][:], in_=den[i][:])
+
+        def finish(g, c, h):
+            i = 4 * g + 2 * c + h
+            for x in range(2):
+                nc.vector.scalar_tensor_tensor(
+                    out=res[i][:, x, :],
+                    in0=acc[h][:, 2 * c + x, :],
+                    scalar=inv[i][:, x : x + 1],
+                    in1=gate[g][:, 2 * h + c, x * E : (x + 1) * E],
+                    op0=ALU.mult,
+                    op1=ALU.mult,
+                )
+            nc.sync.dma_start(
+                out=out[2 * g + h, c * HALF : (c + 1) * HALF, :].rearrange("(p x) e -> p x e", x=2),
+                in_=res[i][:],
+            )
+
+        nc.scalar.dma_start(out=t_sb[:], in_=t.rearrange("(p j) o -> p (j o)", j=PACK))
+        load_k(0)
+        load_q(0, 0)
+        load_q(0, 1)
+        load_v(0)
+        load_k(1)
+        load_q(1, 0)
+        load_og(0)
+        load_q(1, 1)
+        load_v(1)
+        load_og(1)
+        nc.vector.memset(warm_in[:], 0.0)
+        nc.scalar.activation(out=warm_out[:], in_=warm_in[:], func=ACT.Sigmoid)
+
+        deal_k("v", 0, 0, 80)
+        deal_k("s", 0, 80, 128)
+        quant_k(0)
+        deal_q("s", 0, 0, 64)
+        deal_q("v", 0, 64, 128)
+        quant_q(0)
+        scores(0)
+        scores(1)
+        deal_q("v", 1, 0, 128)
+
+        s_extra = {
+            1: [lambda: deal_v("s", 0, 0)],
+            2: [lambda: deal_v("s", 0, 1)],
+            4: [lambda: deal_k("s", 1, 64, 128)],
+            5: [lambda: deal_q("s", 2, 0, 64)],
+            7: [lambda: sigmoid(0, 0), lambda: sigmoid(0, 1)],
+            8: [lambda: deal_q("s", 3, 0, 128)],
+            10: [lambda: deal_v("s", 1, 0), lambda: deal_v("s", 1, 1)],
+            12: [lambda: sigmoid(1, 0)],
+            13: [lambda: sigmoid(1, 1)],
+        }
+        v_extra = {
+            0: [lambda: quant_q(1)],
+            3: [lambda: quant_v(0), lambda: deal_k("v", 1, 0, 64)],
+            4: [lambda: quant_k(1)],
+            5: [lambda: deal_q("v", 2, 64, 128)],
+            6: [lambda: quant_q(2), lambda: denom(0, 0, 0), lambda: denom(0, 0, 1)],
+            7: [lambda: invert(0, 0, 0), lambda: invert(0, 0, 1)],
+            8: [lambda: finish(0, 0, 0), lambda: finish(0, 0, 1)],
+            9: [lambda: quant_q(3), lambda: denom(0, 1, 0), lambda: denom(0, 1, 1)],
+            10: [lambda: invert(0, 1, 0), lambda: invert(0, 1, 1)],
+            11: [lambda: quant_v(1), lambda: finish(0, 1, 0), lambda: finish(0, 1, 1)],
+            13: [lambda: denom(1, 0, 0), lambda: denom(1, 0, 1)],
+            14: [lambda: invert(1, 0, 0), lambda: invert(1, 0, 1)],
+            15: [lambda: finish(1, 0, 0)],
+        }
+        mixes = {4: [0, 1], 5: [2, 3], 6: [4], 7: [5], 8: [6], 9: [7], 12: [8, 9, 10], 13: [11], 14: [12], 15: [13]}
+        for n in range(UNITS):
+            scale(n)
+            for job in s_extra.get(n, []):
+                job()
+            for m in mixes.get(n, []):
+                mix(m)
+            weigh(n)
+            if n > 0:
+                quant_w(n - 1)
+            for job in v_extra.get(n, []):
+                job()
+            if n + 2 < UNITS:
+                scores(n + 2)
+        mix(14)
+        quant_w(15)
+        mix(15)
+        finish(1, 0, 1)
+        denom(1, 1, 0)
+        denom(1, 1, 1)
+        invert(1, 1, 0)
+        invert(1, 1, 1)
+        finish(1, 1, 0)
+        finish(1, 1, 1)

@@ -35,38 +35,47 @@ def tile_rows_a_relu2_gate_kernel(tc, qT, kT, t, v, og, out):
             return [pool.tile(shape, dtype, name=name + str(i)) for i in range(count)]
 
         k_raw = tiles("k_raw", 2, [P, PACK, N], F32)
-        q_raw = tiles("q_raw", 4, [P, PACK, HALF], F32)
+        q_first = sb.tile([P, PACK, P], F32, name="q_first", align_bytes=64)
+        q_second = sb.tile([P, PACK, P], F32, name="q_second", align_bytes=64)
+        q_rest = sb.tile([P, PACK, 2 * P], F32, name="q_rest", align_bytes=64)
+        q_late = tiles("q_late", 2, [P, PACK, HALF], F32)
         v_raw = tiles("v_raw", 2, [P, 2, PACK, E], F32)
-        og_raw = tiles("og_raw", 2, [P, 4, 2 * E], F32)
-        gate = tiles("gate", 2, [P, 4, 2 * E], F32)
+        og_raw = tiles("og_raw", 2, [P, 2, 4, E], F32)
+        gate = tiles("gate", 2, [P, 2, 4, E], F32)
         k_bf = tiles("k_bf", 2, [P, PACK, P, PACK], BF16)
-        q_bf = tiles("q_bf", 4, [P, 2, P, PACK], BF16)
+        q_bf = tiles("q_bf", 2, [P, NQ, PACK], BF16)
         v_bf = tiles("v_bf", 2, [P, 2, E, PACK], BF16)
         k_codes = tiles("k_codes", 2, [P, N], U32)
         k_scales = tiles("k_scales", 2, [P, N], U8)
-        q_codes = tiles("q_codes", 4, [P, HALF], U32)
-        q_scales = tiles("q_scales", 4, [P, HALF], U8)
+        q_codes = tiles("q_codes", 2, [P, NQ], U32)
+        q_scales = tiles("q_scales", 2, [P, NQ], U8)
         v_codes = tiles("v_codes", 2, [P, 2 * E], U32)
         v_scales = tiles("v_scales", 2, [P, 2 * E], U8)
         ta = tiles("ta", UNITS, [P, PACK, P], F32)
-        w_bf = tiles("w_bf", UNITS, [P, P, PACK], BF16)
-        w_codes = tiles("w_codes", UNITS, [P, P], U32)
-        w_scales = tiles("w_scales", UNITS, [P, P], U8)
-        den = tiles("den", 8, [P, 2], F32)
-        inv = tiles("inv", 8, [P, 2], F32)
+        w_bf = sb.tile([P, UNITS, P, PACK], BF16, name="w_bf", align_bytes=64)
+        w_codes = sb.tile([P, UNITS, P], U32, name="w_codes", align_bytes=64)
+        w_scales = sb.tile([P, UNITS, P], U8, name="w_scales", align_bytes=64)
+        groups = [(0, 4), (4, 8), (8, 12), (12, 14), (14, 16)]
+        den = tiles("den", 5, [P, 4], F32)
+        inv = tiles("inv", 5, [P, 4], F32)
         res = tiles("res", 8, [P, 2, E], F32)
         t_sb = sb.tile([P, PACK], F32, name="t_sb", align_bytes=64)
+        t_abs = sb.tile([P, PACK], F32, name="t_abs", align_bytes=64)
+        t_sign = sb.tile([P, PACK], F32, name="t_sign", align_bytes=64)
+        t_half, t_a, t_b, t_c, t_d, t_root = tiles("t_tmp", 6, [P, PACK], F32)
         warm_in = sb.tile([P, 1], F32, name="warm_in", align_bytes=64)
         warm_out = sb.tile([P, 1], F32, name="warm_out", align_bytes=64)
         score = tiles("score", 2 * BANKS, [P, PACK, P], F32, ps)
         acc = tiles("acc", 2, [P, 4, E], F32, ps)
 
-        def load_k(g):
-            nc.sync.dma_start(out=k_raw[g][:], in_=kT[2 * g : 2 * g + 2].rearrange("h (p j) n -> (h p) j n", j=PACK))
+        def rows_of(x, g):
+            return x[2 * g : 2 * g + 2].rearrange("h (p j) n -> (h p) j n", j=PACK)
 
-        def load_q(g, c):
-            rows = qT[2 * g : 2 * g + 2].rearrange("h (p j) n -> (h p) j n", j=PACK)
-            nc.sync.dma_start(out=q_raw[2 * g + c][:], in_=rows[:, :, c * HALF : (c + 1) * HALF])
+        def load_k(g, c0=0, c1=N):
+            nc.sync.dma_start(out=k_raw[g][:, :, c0:c1], in_=rows_of(kT, g)[:, :, c0:c1])
+
+        def load_q(dst, g, c0, c1):
+            nc.sync.dma_start(out=dst[:], in_=rows_of(qT, g)[:, :, c0:c1])
 
         def load_v(g):
             nc.sync.dma_start(
@@ -76,193 +85,321 @@ def tile_rows_a_relu2_gate_kernel(tc, qT, kT, t, v, og, out):
 
         def load_og(g):
             nc.sync.dma_start(
-                out=og_raw[g][:],
-                in_=og[2 * g : 2 * g + 2].rearrange("h (c p x) e -> p (h c) (x e)", c=2, x=2),
+                out=og_raw[g][:].rearrange("p h x e -> p (h x) e"),
+                in_=og[2 * g : 2 * g + 2].rearrange("h (x p) e -> p (h x) e", p=P),
             )
 
         def copy(engine, dst, src):
             if engine == "v":
                 nc.vector.tensor_copy(out=dst, in_=src)
-            else:
+            elif engine == "s":
                 nc.scalar.copy(out=dst, in_=src)
+            else:
+                nc.gpsimd.tensor_scalar(out=dst, in0=src, scalar1=1.0, scalar2=0.0, op0=ALU.mult, op1=ALU.add)
 
         def deal_k(engine, g, s0, s1):
             dst = k_bf[g][:].rearrange("p r s j -> p s j r")
             src = k_raw[g][:].rearrange("p j (s r) -> p s j r", r=PACK)
             copy(engine, dst[:, s0:s1], src[:, s0:s1])
 
-        def deal_q(engine, i, s0, s1):
-            dst = q_bf[i][:].rearrange("p x s j -> p s j x")
-            src = q_raw[i][:].rearrange("p j (s x) -> p s j x", x=2)
-            copy(engine, dst[:, s0:s1], src[:, s0:s1])
+        def q_source(g, c0, c1):
+            if g == 1:
+                return q_late[c0 // HALF][:, :, c0 % HALF : c0 % HALF + c1 - c0]
+            if c0 < P:
+                return q_first[:, :, c0:c1]
+            if c0 < 2 * P:
+                return q_second[:, :, c0 - P : c1 - P]
+            return q_rest[:, :, c0 - 2 * P : c1 - 2 * P]
 
-        def deal_v(engine, g, h):
-            dst = v_bf[g][:, h].rearrange("p (c i) j -> p c j i", i=4)
-            src = v_raw[g][:, h].rearrange("p j (c i) -> p c j i", i=4)
-            copy(engine, dst, src)
+        def deal_q(engine, g, c0, c1):
+            dst = q_bf[g][:, c0:c1, :]
+            src = q_source(g, c0, c1)
+            if engine == "g":
+                copy(engine, dst, src.rearrange("p j n -> p n j"))
+            else:
+                copy(engine, dst.rearrange("p (c i) j -> p c j i", i=2), src.rearrange("p j (c i) -> p c j i", i=2))
+
+        def deal_v(engine, g, h, e0, e1):
+            dst = v_bf[g][:, h, e0:e1, :]
+            src = v_raw[g][:, h, :, e0:e1].rearrange("p j e -> p e j")
+            sign = t_sign[:].unsqueeze(1).to_broadcast([P, e1 - e0, PACK])
+            eng = nc.vector if engine == "v" else nc.gpsimd
+            eng.tensor_tensor(out=dst, in0=src, in1=sign, op=ALU.mult)
 
         def quant(codes, scales, src):
-            nc.vector.quantize_mx(out=codes[:].bitcast(FP8X4), scales=scales[:], in_=src)
+            nc.vector.quantize_mx(out=codes.bitcast(FP8X4), scales=scales, in_=src)
 
         def quant_k(g):
-            quant(k_codes[g], k_scales[g], k_bf[g][:].rearrange("p r s j -> p (r s j)"))
+            quant(k_codes[g][:], k_scales[g][:], k_bf[g][:].rearrange("p r s j -> p (r s j)"))
 
-        def quant_q(i):
-            quant(q_codes[i], q_scales[i], q_bf[i][:].rearrange("p x s j -> p (x s j)"))
+        def quant_q(g, c0, c1):
+            quant(q_codes[g][:, c0:c1], q_scales[g][:, c0:c1], q_bf[g][:, c0:c1, :].rearrange("p n j -> p (n j)"))
 
         def quant_v(g):
-            quant(v_codes[g], v_scales[g], v_bf[g][:].rearrange("p h e j -> p (h e j)"))
+            quant(v_codes[g][:], v_scales[g][:], v_bf[g][:].rearrange("p h e j -> p (h e j)"))
 
-        def quant_w(n):
-            quant(w_codes[n], w_scales[n], w_bf[n][:].rearrange("p s j -> p (s j)"))
-
-        def parts(n):
-            return n // 8, (n // 4) % 2, (n // 2) % 2, n % 2
+        def quant_w(n0, n1):
+            quant(
+                w_codes[:, n0:n1, :].rearrange("p n s -> p (n s)"),
+                w_scales[:, n0:n1, :].rearrange("p n s -> p (n s)"),
+                w_bf[:, n0:n1].rearrange("p n s j -> p (n s j)"),
+            )
 
         def bank(n):
             return score[(n % 2) * BANKS + (n // 2) % BANKS]
 
-        def scores(n):
-            g, c, x, h = parts(n)
-            rows = slice(h * ROWS, (h + 1) * ROWS)
+        def scores(m):
+            g, x = m // 4, m % 4
             cols = slice(x * P, (x + 1) * P)
             for r in range(PACK):
                 keys = slice(r * P, (r + 1) * P)
-                nc.tensor.matmul_mx(
-                    out=bank(n)[:, r, :],
-                    lhsT=k_codes[g][rows, keys].bitcast(FP8X4),
-                    lhsT_scale=k_scales[g][rows, keys],
-                    rhs=q_codes[2 * g + c][rows, cols].bitcast(FP8X4),
-                    rhs_scale=q_scales[2 * g + c][rows, cols],
-                    start=True,
-                    stop=True,
+                for h in range(2):
+                    rows = slice(h * ROWS, (h + 1) * ROWS)
+                    nc.tensor.matmul_mx(
+                        out=bank(2 * m + h)[:, r, :],
+                        lhsT=k_codes[g][rows, keys].bitcast(FP8X4),
+                        lhsT_scale=k_scales[g][rows, keys],
+                        rhs=q_codes[g][rows, cols].bitcast(FP8X4),
+                        rhs_scale=q_scales[g][rows, cols],
+                        start=True,
+                        stop=True,
+                    )
+
+        def rectify(engine, n):
+            if engine == "v":
+                nc.vector.scalar_tensor_tensor(
+                    out=ta[n][:].rearrange("p r s -> p (r s)").rearrange("p (s r) -> p s r", r=PACK),
+                    in0=bank(n)[:].rearrange("p r s -> p s r"),
+                    scalar=0.0,
+                    in1=t_root[:].unsqueeze(1).to_broadcast([P, P, PACK]),
+                    op0=ALU.max,
+                    op1=ALU.mult,
+                )
+            else:
+                for r in range(PACK):
+                    nc.scalar.activation(out=ta[n][:, r, :], in_=bank(n)[:, r, :], func=ACT.Relu, scale=t_root[:, r : r + 1])
+
+        def square(engine, n):
+            if engine == "v":
+                nc.scalar.activation(
+                    out=w_bf[:, n].rearrange("p s r -> p (s r)"), in_=ta[n][:].rearrange("p r s -> p (r s)"), func=ACT.Square
+                )
+            else:
+                nc.scalar.activation(
+                    out=w_bf[:, n].rearrange("p (c i) r -> p c r i", i=2),
+                    in_=ta[n][:].rearrange("p r (c i) -> p c r i", i=2),
+                    func=ACT.Square,
                 )
 
-        def scale(n):
-            for r in range(PACK):
-                nc.scalar.activation(out=ta[n][:, r, :], in_=bank(n)[:, r, :], func=ACT.Copy, scale=t_sb[:, r : r + 1])
+        def load_t():
+            nc.scalar.dma_start(out=t_sb[:], in_=t.rearrange("(p j) o -> p (j o)", j=PACK))
 
-        def weigh(n):
-            nc.vector.scalar_tensor_tensor(
-                out=w_bf[n][:],
-                in0=bank(n)[:].rearrange("p r s -> p s r"),
-                scalar=0.0,
-                in1=ta[n][:].rearrange("p r s -> p s r"),
-                op0=ALU.max,
-                op1=ALU.mult,
-            )
+        def prep(i):
+            if i == 0:
+                nc.vector.memset(warm_in[:], 0.0)
+            elif i == 1:
+                nc.vector.scalar_tensor_tensor(out=t_abs[:], in0=t_sb[:], scalar=-1.0, in1=t_sb[:], op0=ALU.mult, op1=ALU.max)
+            elif i == 2:
+                nc.scalar.activation(out=t_half[:], in_=t_abs[:], func=ACT.Sqrt, scale=0.25)
+            elif i == 3:
+                nc.scalar.activation(out=warm_out[:], in_=warm_in[:], func=ACT.Sigmoid)
+            elif i == 4:
+                nc.vector.tensor_scalar_max(out=t_a[:], in0=t_half[:], scalar1=1e-30)
+            elif i == 5:
+                nc.vector.reciprocal(out=t_b[:], in_=t_a[:])
+            elif i == 6:
+                nc.vector.scalar_tensor_tensor(out=t_c[:], in0=t_b[:], scalar=0.25, in1=t_abs[:], op0=ALU.mult, op1=ALU.mult)
+            elif i == 7:
+                nc.vector.tensor_tensor(out=t_root[:], in0=t_c[:], in1=t_half[:], op=ALU.add)
+            elif i == 8:
+                nc.vector.tensor_scalar(out=t_d[:], in0=t_sb[:], scalar1=0.0, scalar2=2.0, op0=ALU.is_ge, op1=ALU.mult)
+            else:
+                nc.vector.tensor_scalar_add(out=t_sign[:], in0=t_d[:], scalar1=-1.0)
+
+        def slot(n):
+            if n >= 14:
+                return acc[0], n - 14
+            return acc[(n // 4) % 2], n % 4
 
         def mix(n):
-            g, c, x, h = parts(n)
+            g, h = n // 8, n % 2
             cols = slice(h * E, (h + 1) * E)
+            tile, i = slot(n)
             nc.tensor.matmul_mx(
-                out=acc[h][:, 2 * c + x, :],
-                lhsT=w_codes[n][:].bitcast(FP8X4),
-                lhsT_scale=w_scales[n][:],
+                out=tile[:, i, :],
+                lhsT=w_codes[:, n, :].bitcast(FP8X4),
+                lhsT_scale=w_scales[:, n, :],
                 rhs=v_codes[g][:, cols].bitcast(FP8X4),
                 rhs_scale=v_scales[g][:, cols],
                 start=True,
                 stop=True,
             )
 
-        def sigmoid(g, h):
-            nc.scalar.activation(out=gate[g][:, 2 * h : 2 * h + 2, :], in_=og_raw[g][:, 2 * h : 2 * h + 2, :], func=ACT.Sigmoid)
+        def sigmoid(g, c):
+            nc.scalar.activation(
+                out=gate[g][:, :, 2 * c : 2 * c + 2, :], in_=og_raw[g][:, :, 2 * c : 2 * c + 2, :], func=ACT.Sigmoid
+            )
 
-        def denom(g, c, h):
-            i = 4 * g + 2 * c + h
-            nc.vector.tensor_scalar_add(out=den[i][:], in0=acc[h][:, 2 * c : 2 * c + 2, E - 1], scalar1=1.0)
+        def denom(i):
+            n0, n1 = groups[i]
+            tile, first = slot(n0)
+            nc.vector.tensor_scalar_add(out=den[i][:, : n1 - n0], in0=tile[:, first : first + n1 - n0, E - 1], scalar1=1.0)
 
-        def invert(g, c, h):
-            i = 4 * g + 2 * c + h
-            nc.vector.reciprocal(out=inv[i][:], in_=den[i][:])
+        def invert(i):
+            n0, n1 = groups[i]
+            nc.vector.reciprocal(out=inv[i][:, : n1 - n0], in_=den[i][:, : n1 - n0])
 
-        def finish(g, c, h):
-            i = 4 * g + 2 * c + h
-            for x in range(2):
+        def finish(m):
+            g, x = m // 4, m % 4
+            i = [j for j, (n0, n1) in enumerate(groups) if n0 <= 2 * m < n1][0]
+            for h in range(2):
+                n = 2 * m + h
+                tile, place = slot(n)
+                col = n - groups[i][0]
                 nc.vector.scalar_tensor_tensor(
-                    out=res[i][:, x, :],
-                    in0=acc[h][:, 2 * c + x, :],
-                    scalar=inv[i][:, x : x + 1],
-                    in1=gate[g][:, 2 * h + c, x * E : (x + 1) * E],
+                    out=res[m][:, h, :],
+                    in0=tile[:, place, :],
+                    scalar=inv[i][:, col : col + 1],
+                    in1=gate[g][:, h, x, :],
                     op0=ALU.mult,
                     op1=ALU.mult,
                 )
             nc.sync.dma_start(
-                out=out[2 * g + h, c * HALF : (c + 1) * HALF, :].rearrange("(p x) e -> p x e", x=2),
-                in_=res[i][:],
+                out=out[2 * g : 2 * g + 2, x * P : (x + 1) * P, :].rearrange("h p e -> p h e"),
+                in_=res[m][:],
             )
 
-        nc.scalar.dma_start(out=t_sb[:], in_=t.rearrange("(p j) o -> p (j o)", j=PACK))
+        load_t()
         load_k(0)
-        load_q(0, 0)
-        load_q(0, 1)
-        load_v(0)
+        load_q(q_first, 0, 0, P)
+        load_q(q_second, 0, P, 2 * P)
+        load_q(q_rest, 0, 2 * P, NQ)
         load_k(1)
-        load_q(1, 0)
+        load_q(q_late[0], 1, 0, HALF)
+        load_v(0)
+        load_q(q_late[1], 1, HALF, NQ)
         load_og(0)
-        load_q(1, 1)
         load_v(1)
         load_og(1)
-        nc.vector.memset(warm_in[:], 0.0)
-        nc.scalar.activation(out=warm_out[:], in_=warm_in[:], func=ACT.Sigmoid)
-
-        deal_k("v", 0, 0, 80)
-        deal_k("s", 0, 80, 128)
+        prep(0)
+        prep(1)
+        prep(2)
+        prep(3)
+        prep(4)
+        deal_k("s", 0, 0, 32)
+        prep(5)
+        prep(6)
+        prep(7)
+        prep(8)
+        deal_k("v", 0, 32, 128)
+        deal_q("s", 0, 0, 128)
+        prep(9)
+        deal_q("s", 0, 128, 256)
         quant_k(0)
-        deal_q("s", 0, 0, 64)
-        deal_q("v", 0, 64, 128)
-        quant_q(0)
+        quant_q(0, 0, 128)
+        quant_q(0, 128, 256)
+        deal_q("v", 0, 256, 384)
         scores(0)
         scores(1)
-        deal_q("v", 1, 0, 128)
-
-        s_extra = {
-            1: [lambda: deal_v("s", 0, 0)],
-            2: [lambda: deal_v("s", 0, 1)],
-            4: [lambda: deal_k("s", 1, 64, 128)],
-            5: [lambda: deal_q("s", 2, 0, 64)],
-            7: [lambda: sigmoid(0, 0), lambda: sigmoid(0, 1)],
-            8: [lambda: deal_q("s", 3, 0, 128)],
-            10: [lambda: deal_v("s", 1, 0), lambda: deal_v("s", 1, 1)],
-            12: [lambda: sigmoid(1, 0)],
-            13: [lambda: sigmoid(1, 1)],
-        }
-        v_extra = {
-            0: [lambda: quant_q(1)],
-            3: [lambda: quant_v(0), lambda: deal_k("v", 1, 0, 64)],
-            4: [lambda: quant_k(1)],
-            5: [lambda: deal_q("v", 2, 64, 128)],
-            6: [lambda: quant_q(2), lambda: denom(0, 0, 0), lambda: denom(0, 0, 1)],
-            7: [lambda: invert(0, 0, 0), lambda: invert(0, 0, 1)],
-            8: [lambda: finish(0, 0, 0), lambda: finish(0, 0, 1)],
-            9: [lambda: quant_q(3), lambda: denom(0, 1, 0), lambda: denom(0, 1, 1)],
-            10: [lambda: invert(0, 1, 0), lambda: invert(0, 1, 1)],
-            11: [lambda: quant_v(1), lambda: finish(0, 1, 0), lambda: finish(0, 1, 1)],
-            13: [lambda: denom(1, 0, 0), lambda: denom(1, 0, 1)],
-            14: [lambda: invert(1, 0, 0), lambda: invert(1, 0, 1)],
-            15: [lambda: finish(1, 0, 0)],
-        }
-        mixes = {4: [0, 1], 5: [2, 3], 6: [4], 7: [5], 8: [6], 9: [7], 12: [8, 9, 10], 13: [11], 14: [12], 15: [13]}
-        for n in range(UNITS):
-            scale(n)
-            for job in s_extra.get(n, []):
-                job()
-            for m in mixes.get(n, []):
-                mix(m)
-            weigh(n)
-            if n > 0:
-                quant_w(n - 1)
-            for job in v_extra.get(n, []):
-                job()
-            if n + 2 < UNITS:
-                scores(n + 2)
+        deal_q("s", 0, 384, 512)
+        rectify("v", 0)
+        rectify("s", 1)
+        quant_q(0, 256, 512)
+        square("v", 0)
+        rectify("v", 2)
+        scores(2)
+        square("s", 1)
+        square("v", 2)
+        scores(3)
+        rectify("v", 3)
+        deal_k("v", 1, 0, 96)
+        rectify("s", 4)
+        square("v", 3)
+        rectify("v", 5)
+        rectify("v", 6)
+        deal_q("s", 1, 0, 128)
+        deal_q("v", 1, 128, 256)
+        deal_k("v", 1, 96, 128)
+        square("s", 4)
+        quant_q(1, 0, 256)
+        quant_k(1)
+        deal_v("v", 0, 0, 0, 128)
+        rectify("s", 7)
+        square("v", 5)
+        deal_v("v", 0, 1, 0, 64)
+        deal_q("v", 1, 256, 384)
+        deal_q("s", 1, 384, 512)
+        square("v", 6)
+        quant_w(0, 4)
+        deal_v("v", 0, 1, 64, 128)
+        scores(4)
+        scores(5)
+        quant_q(1, 256, 512)
+        square("s", 7)
+        rectify("v", 8)
+        quant_v(0)
+        scores(6)
+        rectify("v", 9)
+        mix(0)
+        rectify("v", 10)
+        rectify("s", 11)
+        sigmoid(0, 0)
+        mix(1)
+        mix(2)
+        quant_w(4, 8)
+        mix(3)
+        denom(0)
+        deal_v("v", 1, 0, 0, 64)
+        invert(0)
+        mix(4)
+        square("v", 8)
+        deal_v("v", 1, 0, 64, 128)
+        square("v", 9)
+        quant_w(8, 10)
+        mix(5)
+        rectify("s", 12)
+        deal_v("v", 1, 1, 0, 128)
+        mix(6)
+        sigmoid(0, 1)
+        scores(7)
+        finish(0)
+        square("v", 10)
+        rectify("v", 13)
+        mix(7)
+        denom(1)
+        quant_v(1)
+        finish(1)
+        square("s", 11)
+        square("s", 12)
+        mix(8)
+        square("v", 13)
+        quant_w(10, 12)
+        mix(9)
+        invert(1)
+        sigmoid(1, 0)
+        rectify("v", 14)
+        mix(10)
+        mix(11)
+        finish(2)
+        rectify("s", 15)
+        denom(2)
+        square("v", 14)
+        finish(3)
+        square("s", 15)
+        sigmoid(1, 1)
+        invert(2)
+        quant_w(12, 14)
+        finish(4)
+        finish(5)
+        quant_w(14, 15)
+        mix(12)
+        mix(13)
+        denom(3)
+        quant_w(15, 16)
         mix(14)
-        quant_w(15)
+        invert(3)
         mix(15)
-        finish(1, 0, 1)
-        denom(1, 1, 0)
-        denom(1, 1, 1)
-        invert(1, 1, 0)
-        invert(1, 1, 1)
-        finish(1, 1, 0)
-        finish(1, 1, 1)
+        finish(6)
+        denom(4)
+        invert(4)
+        finish(7)

@@ -17,9 +17,14 @@ P = 128
 PACK = 4
 ROWS = 64
 PAIRS = 2
-HALF = 256
-UNITS = 16
-BANKS = 3
+TILES = NQ // P
+HALF = NQ // 2
+UNITS = H * TILES
+SCORE_BANKS = 3
+GROUPS = [(0, 4), (4, 8), (8, 12), (12, 14), (14, 16)]
+ON_SCALAR = (1, 13)
+KEY_SPLIT = (80, 48)
+TINY = 1e-30
 
 
 def tile_rows_a_relu2_gate_kernel(tc, qT, kT, t, v, og, out):
@@ -29,58 +34,49 @@ def tile_rows_a_relu2_gate_kernel(tc, qT, kT, t, v, og, out):
         ps = ctx.enter_context(tc.psum_pool(name="ps", bufs=1))
         ctx.enter_context(tc.manual_schedule())
 
-        def tiles(name, count, shape, dtype, pool=sb):
-            if pool is sb:
-                return [pool.tile(shape, dtype, name=name + str(i), align_bytes=64) for i in range(count)]
-            return [pool.tile(shape, dtype, name=name + str(i)) for i in range(count)]
+        def tiles(name, count, shape, dtype):
+            return [sb.tile(shape, dtype, name=name + str(i), align_bytes=64) for i in range(count)]
 
-        k_raw = tiles("k_raw", 2, [P, PACK, N], F32)
-        q_first = sb.tile([P, PACK, P], F32, name="q_first", align_bytes=64)
-        q_second = sb.tile([P, PACK, P], F32, name="q_second", align_bytes=64)
-        q_rest = sb.tile([P, PACK, 2 * P], F32, name="q_rest", align_bytes=64)
-        q_late = tiles("q_late", 2, [P, PACK, HALF], F32)
-        v_raw = tiles("v_raw", 2, [P, 2, PACK, E], F32)
-        og_raw = tiles("og_raw", 2, [P, 2, 4, E], F32)
-        gate = tiles("gate", 2, [P, 2, 4, E], F32)
-        k_bf = tiles("k_bf", 2, [P, PACK, P, PACK], BF16)
-        q_bf = tiles("q_bf", 2, [P, NQ, PACK], BF16)
-        v_bf = tiles("v_bf", 2, [P, 2, E, PACK], BF16)
-        k_codes = tiles("k_codes", 2, [P, N], U32)
-        k_scales = tiles("k_scales", 2, [P, N], U8)
-        q_codes = tiles("q_codes", 2, [P, NQ], U32)
-        q_scales = tiles("q_scales", 2, [P, NQ], U8)
-        v_codes = tiles("v_codes", 2, [P, 2 * E], U32)
-        v_scales = tiles("v_scales", 2, [P, 2 * E], U8)
-        ta = tiles("ta", UNITS, [P, PACK, P], F32)
+        k_raw = tiles("k_raw", PAIRS, [P, PACK, N], F32)
+        q_raw = tiles("q_raw", 2 * PAIRS, [P, PACK, HALF], F32)
+        v_raw = tiles("v_raw", PAIRS, [P, 2, PACK, E], F32)
+        og_raw = tiles("og_raw", PAIRS, [P, 2, TILES, E], F32)
+        gate = tiles("gate", PAIRS, [P, 2, TILES, E], F32)
+        k_bf = tiles("k_bf", PAIRS, [P, PACK, P, PACK], BF16)
+        q_bf = tiles("q_bf", PAIRS, [P, NQ, PACK], BF16)
+        v_bf = tiles("v_bf", PAIRS, [P, 2, E, PACK], BF16)
+        k_codes = tiles("k_codes", PAIRS, [P, N], U32)
+        k_scales = tiles("k_scales", PAIRS, [P, N], U8)
+        q_codes = tiles("q_codes", PAIRS, [P, NQ], U32)
+        q_scales = tiles("q_scales", PAIRS, [P, NQ], U8)
+        v_codes = tiles("v_codes", PAIRS, [P, 2 * E], U32)
+        v_scales = tiles("v_scales", PAIRS, [P, 2 * E], U8)
+        root_w = tiles("root_w", UNITS, [P, PACK * P], F32)
         w_bf = sb.tile([P, UNITS, P, PACK], BF16, name="w_bf", align_bytes=64)
         w_codes = sb.tile([P, UNITS, P], U32, name="w_codes", align_bytes=64)
         w_scales = sb.tile([P, UNITS, P], U8, name="w_scales", align_bytes=64)
-        groups = [(0, 4), (4, 8), (8, 12), (12, 14), (14, 16)]
-        den = tiles("den", 5, [P, 4], F32)
-        inv = tiles("inv", 5, [P, 4], F32)
-        res = tiles("res", 8, [P, 2, E], F32)
-        t_sb = sb.tile([P, PACK], F32, name="t_sb", align_bytes=64)
-        t_abs = sb.tile([P, PACK], F32, name="t_abs", align_bytes=64)
-        t_sign = sb.tile([P, PACK], F32, name="t_sign", align_bytes=64)
-        t_half, t_a, t_b, t_c, t_d, t_root = tiles("t_tmp", 6, [P, PACK], F32)
-        warm_in = sb.tile([P, 1], F32, name="warm_in", align_bytes=64)
-        warm_out = sb.tile([P, 1], F32, name="warm_out", align_bytes=64)
-        score = tiles("score", 2 * BANKS, [P, PACK, P], F32, ps)
-        acc = tiles("acc", 2, [P, 4, E], F32, ps)
+        den = tiles("den", len(GROUPS), [P, 4], F32)
+        inv = tiles("inv", len(GROUPS), [P, 4], F32)
+        res = tiles("res", UNITS // 2, [P, 2, E], F32)
+        t_sb, t_abs, half_root, guarded, recip, step, t_root, twice_pos = tiles("t_work", 8, [P, PACK], F32)
+        t_sign = tiles("t_sign", PAIRS, [P, PACK], F32)
+        warm_in, warm_out = tiles("warm", 2, [P, 1], F32)
+        score = [ps.tile([P, PACK, P], F32, name="score" + str(i)) for i in range(2 * SCORE_BANKS)]
+        y_bank = [ps.tile([P, 4, E], F32, name="y_bank" + str(i)) for i in range(2)]
 
-        def rows_of(x, g):
+        def feature_rows(x, g):
             return x[2 * g : 2 * g + 2].rearrange("h (p j) n -> (h p) j n", j=PACK)
 
-        def load_k(g, c0=0, c1=N):
-            nc.sync.dma_start(out=k_raw[g][:, :, c0:c1], in_=rows_of(kT, g)[:, :, c0:c1])
+        def load_k(g):
+            nc.sync.dma_start(out=k_raw[g][:], in_=feature_rows(kT, g))
 
-        def load_q(dst, g, c0, c1):
-            nc.sync.dma_start(out=dst[:], in_=rows_of(qT, g)[:, :, c0:c1])
+        def load_q(g, c):
+            nc.sync.dma_start(out=q_raw[2 * g + c][:], in_=feature_rows(qT, g)[:, :, c * HALF : (c + 1) * HALF])
 
         def load_v(g):
             nc.sync.dma_start(
-                out=v_raw[g][:].rearrange("p h j e -> p h (j e)"),
-                in_=v[2 * g : 2 * g + 2].rearrange("h (p j) e -> p h (j e)", j=PACK),
+                out=v_raw[g][:].rearrange("s h r e -> s h (r e)"),
+                in_=v[2 * g : 2 * g + 2].rearrange("h (s r) e -> s h (r e)", r=PACK),
             )
 
         def load_og(g):
@@ -89,176 +85,144 @@ def tile_rows_a_relu2_gate_kernel(tc, qT, kT, t, v, og, out):
                 in_=og[2 * g : 2 * g + 2].rearrange("h (x p) e -> p (h x) e", p=P),
             )
 
-        def copy(engine, dst, src):
-            if engine == "v":
-                nc.vector.tensor_copy(out=dst, in_=src)
-            elif engine == "s":
+        def copy(on_scalar, dst, src):
+            if on_scalar:
                 nc.scalar.copy(out=dst, in_=src)
             else:
-                nc.gpsimd.tensor_scalar(out=dst, in0=src, scalar1=1.0, scalar2=0.0, op0=ALU.mult, op1=ALU.add)
+                nc.vector.tensor_copy(out=dst, in_=src)
 
-        def deal_k(engine, g, s0, s1):
+        def pack_k(g):
             dst = k_bf[g][:].rearrange("p r s j -> p s j r")
             src = k_raw[g][:].rearrange("p j (s r) -> p s j r", r=PACK)
-            copy(engine, dst[:, s0:s1], src[:, s0:s1])
+            copy(False, dst[:, : KEY_SPLIT[g]], src[:, : KEY_SPLIT[g]])
+            copy(True, dst[:, KEY_SPLIT[g] :], src[:, KEY_SPLIT[g] :])
 
-        def q_source(g, c0, c1):
-            if g == 1:
-                return q_late[c0 // HALF][:, :, c0 % HALF : c0 % HALF + c1 - c0]
-            if c0 < P:
-                return q_first[:, :, c0:c1]
-            if c0 < 2 * P:
-                return q_second[:, :, c0 - P : c1 - P]
-            return q_rest[:, :, c0 - 2 * P : c1 - 2 * P]
-
-        def deal_q(engine, g, c0, c1):
-            dst = q_bf[g][:, c0:c1, :]
-            src = q_source(g, c0, c1)
-            if engine == "g":
-                copy(engine, dst, src.rearrange("p j n -> p n j"))
-            else:
-                copy(engine, dst.rearrange("p (c i) j -> p c j i", i=2), src.rearrange("p j (c i) -> p c j i", i=2))
-
-        def deal_v(engine, g, h, e0, e1):
-            dst = v_bf[g][:, h, e0:e1, :]
-            src = v_raw[g][:, h, :, e0:e1].rearrange("p j e -> p e j")
-            sign = t_sign[:].unsqueeze(1).to_broadcast([P, e1 - e0, PACK])
-            eng = nc.vector if engine == "v" else nc.gpsimd
-            eng.tensor_tensor(out=dst, in0=src, in1=sign, op=ALU.mult)
-
-        def quant(codes, scales, src):
-            nc.vector.quantize_mx(out=codes.bitcast(FP8X4), scales=scales, in_=src)
-
-        def quant_k(g):
-            quant(k_codes[g][:], k_scales[g][:], k_bf[g][:].rearrange("p r s j -> p (r s j)"))
-
-        def quant_q(g, c0, c1):
-            quant(q_codes[g][:, c0:c1], q_scales[g][:, c0:c1], q_bf[g][:, c0:c1, :].rearrange("p n j -> p (n j)"))
-
-        def quant_v(g):
-            quant(v_codes[g][:], v_scales[g][:], v_bf[g][:].rearrange("p h e j -> p (h e j)"))
-
-        def quant_w(n0, n1):
-            quant(
-                w_codes[:, n0:n1, :].rearrange("p n s -> p (n s)"),
-                w_scales[:, n0:n1, :].rearrange("p n s -> p (n s)"),
-                w_bf[:, n0:n1].rearrange("p n s j -> p (n s j)"),
+        def pack_q(g, c0, c1, on_scalar):
+            src = q_raw[2 * g + c0 // HALF][:, :, c0 % HALF : c0 % HALF + c1 - c0]
+            copy(
+                on_scalar,
+                q_bf[g][:, c0:c1, :].rearrange("p (c i) j -> p c j i", i=2),
+                src.rearrange("p j (c i) -> p c j i", i=2),
             )
 
-        def bank(n):
-            return score[(n % 2) * BANKS + (n // 2) % BANKS]
+        def pack_v(g):
+            nc.vector.tensor_scalar_add(out=t_sign[g][:], in0=twice_pos[:], scalar1=-1.0)
+            for h in range(2):
+                nc.gpsimd.tensor_tensor(
+                    out=v_bf[g][:, h],
+                    in0=v_raw[g][:, h].rearrange("s r e -> s e r"),
+                    in1=t_sign[g][:].unsqueeze(1).to_broadcast([P, E, PACK]),
+                    op=ALU.mult,
+                )
+
+        def quantize(codes, scales, src):
+            nc.vector.quantize_mx(out=codes.bitcast(FP8X4), scales=scales, in_=src)
+
+        def quantize_k(g):
+            quantize(k_codes[g][:], k_scales[g][:], k_bf[g][:].rearrange("p r s j -> p (r s j)"))
+
+        def quantize_q(g, c0, c1):
+            quantize(q_codes[g][:, c0:c1], q_scales[g][:, c0:c1], q_bf[g][:, c0:c1, :].rearrange("p n j -> p (n j)"))
+
+        def quantize_v(g):
+            quantize(v_codes[g][:], v_scales[g][:], v_bf[g][:].rearrange("s h e r -> s (h e r)"))
+
+        def quantize_w(n0, n1):
+            quantize(
+                w_codes[:, n0:n1, :].rearrange("s n q -> s (n q)"),
+                w_scales[:, n0:n1, :].rearrange("s n q -> s (n q)"),
+                w_bf[:, n0:n1].rearrange("s n q r -> s (n q r)"),
+            )
+
+        def score_bank(n):
+            return score[(n % 2) * SCORE_BANKS + (n // 2) % SCORE_BANKS]
 
         def scores(m):
-            g, x = m // 4, m % 4
-            cols = slice(x * P, (x + 1) * P)
+            g, x = divmod(m, TILES)
+            queries = slice(x * P, (x + 1) * P)
             for r in range(PACK):
                 keys = slice(r * P, (r + 1) * P)
                 for h in range(2):
                     rows = slice(h * ROWS, (h + 1) * ROWS)
                     nc.tensor.matmul_mx(
-                        out=bank(2 * m + h)[:, r, :],
+                        out=score_bank(2 * m + h)[:, r, :],
                         lhsT=k_codes[g][rows, keys].bitcast(FP8X4),
                         lhsT_scale=k_scales[g][rows, keys],
-                        rhs=q_codes[g][rows, cols].bitcast(FP8X4),
-                        rhs_scale=q_scales[g][rows, cols],
+                        rhs=q_codes[g][rows, queries].bitcast(FP8X4),
+                        rhs_scale=q_scales[g][rows, queries],
                         start=True,
                         stop=True,
                     )
 
-        def rectify(engine, n):
-            if engine == "v":
+        def rectify(n):
+            if n in ON_SCALAR:
+                for r in range(PACK):
+                    nc.scalar.activation(
+                        out=root_w[n][:, r * P : (r + 1) * P],
+                        in_=score_bank(n)[:, r, :],
+                        func=ACT.Relu,
+                        scale=t_root[:, r : r + 1],
+                    )
+            else:
                 nc.vector.scalar_tensor_tensor(
-                    out=ta[n][:].rearrange("p r s -> p (r s)").rearrange("p (s r) -> p s r", r=PACK),
-                    in0=bank(n)[:].rearrange("p r s -> p s r"),
+                    out=root_w[n][:].rearrange("s (q r) -> s q r", r=PACK),
+                    in0=score_bank(n)[:].rearrange("s r q -> s q r"),
                     scalar=0.0,
                     in1=t_root[:].unsqueeze(1).to_broadcast([P, P, PACK]),
                     op0=ALU.max,
                     op1=ALU.mult,
                 )
-            else:
-                for r in range(PACK):
-                    nc.scalar.activation(out=ta[n][:, r, :], in_=bank(n)[:, r, :], func=ACT.Relu, scale=t_root[:, r : r + 1])
 
-        def square(engine, n):
-            if engine == "v":
-                nc.scalar.activation(
-                    out=w_bf[:, n].rearrange("p s r -> p (s r)"), in_=ta[n][:].rearrange("p r s -> p (r s)"), func=ACT.Square
+        def square(n):
+            if n in ON_SCALAR:
+                dst = w_bf[:, n].rearrange("s (c i) r -> s c r i", i=2)
+                src = root_w[n][:].rearrange("s (r c i) -> s c r i", r=PACK, i=2)
+            else:
+                dst = w_bf[:, n].rearrange("s q r -> s (q r)")
+                src = root_w[n][:]
+            nc.scalar.activation(out=dst, in_=src, func=ACT.Square)
+
+        def group_of(n):
+            return [i for i, (n0, n1) in enumerate(GROUPS) if n0 <= n < n1][0]
+
+        def y_of(n0, n1):
+            i = group_of(n0)
+            return y_bank[i % 2][:, n0 - GROUPS[i][0] : n1 - GROUPS[i][0], :]
+
+        def mix(n0, n1):
+            for n in range(n0, n1):
+                cols = slice((n % 2) * E, (n % 2 + 1) * E)
+                nc.tensor.matmul_mx(
+                    out=y_of(n, n + 1)[:, 0, :],
+                    lhsT=w_codes[:, n, :].bitcast(FP8X4),
+                    lhsT_scale=w_scales[:, n, :],
+                    rhs=v_codes[n // 8][:, cols].bitcast(FP8X4),
+                    rhs_scale=v_scales[n // 8][:, cols],
+                    start=True,
+                    stop=True,
                 )
-            else:
-                nc.scalar.activation(
-                    out=w_bf[:, n].rearrange("p (c i) r -> p c r i", i=2),
-                    in_=ta[n][:].rearrange("p r (c i) -> p c r i", i=2),
-                    func=ACT.Square,
-                )
-
-        def load_t():
-            nc.scalar.dma_start(out=t_sb[:], in_=t.rearrange("(p j) o -> p (j o)", j=PACK))
-
-        def prep(i):
-            if i == 0:
-                nc.vector.memset(warm_in[:], 0.0)
-            elif i == 1:
-                nc.vector.scalar_tensor_tensor(out=t_abs[:], in0=t_sb[:], scalar=-1.0, in1=t_sb[:], op0=ALU.mult, op1=ALU.max)
-            elif i == 2:
-                nc.scalar.activation(out=t_half[:], in_=t_abs[:], func=ACT.Sqrt, scale=0.25)
-            elif i == 3:
-                nc.scalar.activation(out=warm_out[:], in_=warm_in[:], func=ACT.Sigmoid)
-            elif i == 4:
-                nc.vector.tensor_scalar_max(out=t_a[:], in0=t_half[:], scalar1=1e-30)
-            elif i == 5:
-                nc.vector.reciprocal(out=t_b[:], in_=t_a[:])
-            elif i == 6:
-                nc.vector.scalar_tensor_tensor(out=t_c[:], in0=t_b[:], scalar=0.25, in1=t_abs[:], op0=ALU.mult, op1=ALU.mult)
-            elif i == 7:
-                nc.vector.tensor_tensor(out=t_root[:], in0=t_c[:], in1=t_half[:], op=ALU.add)
-            elif i == 8:
-                nc.vector.tensor_scalar(out=t_d[:], in0=t_sb[:], scalar1=0.0, scalar2=2.0, op0=ALU.is_ge, op1=ALU.mult)
-            else:
-                nc.vector.tensor_scalar_add(out=t_sign[:], in0=t_d[:], scalar1=-1.0)
-
-        def slot(n):
-            if n >= 14:
-                return acc[0], n - 14
-            return acc[(n // 4) % 2], n % 4
-
-        def mix(n):
-            g, h = n // 8, n % 2
-            cols = slice(h * E, (h + 1) * E)
-            tile, i = slot(n)
-            nc.tensor.matmul_mx(
-                out=tile[:, i, :],
-                lhsT=w_codes[:, n, :].bitcast(FP8X4),
-                lhsT_scale=w_scales[:, n, :],
-                rhs=v_codes[g][:, cols].bitcast(FP8X4),
-                rhs_scale=v_scales[g][:, cols],
-                start=True,
-                stop=True,
-            )
 
         def sigmoid(g, c):
-            nc.scalar.activation(
-                out=gate[g][:, :, 2 * c : 2 * c + 2, :], in_=og_raw[g][:, :, 2 * c : 2 * c + 2, :], func=ACT.Sigmoid
-            )
+            tiles_c = slice(2 * c, 2 * c + 2)
+            nc.scalar.activation(out=gate[g][:, :, tiles_c, :], in_=og_raw[g][:, :, tiles_c, :], func=ACT.Sigmoid)
 
-        def denom(i):
-            n0, n1 = groups[i]
-            tile, first = slot(n0)
-            nc.vector.tensor_scalar_add(out=den[i][:, : n1 - n0], in0=tile[:, first : first + n1 - n0, E - 1], scalar1=1.0)
+        def denominator(i):
+            n0, n1 = GROUPS[i]
+            nc.vector.tensor_scalar_add(out=den[i][:, : n1 - n0], in0=y_of(n0, n1)[:, :, E - 1], scalar1=1.0)
 
         def invert(i):
-            n0, n1 = groups[i]
+            n0, n1 = GROUPS[i]
             nc.vector.reciprocal(out=inv[i][:, : n1 - n0], in_=den[i][:, : n1 - n0])
 
         def finish(m):
-            g, x = m // 4, m % 4
-            i = [j for j, (n0, n1) in enumerate(groups) if n0 <= 2 * m < n1][0]
+            g, x = divmod(m, TILES)
+            i = group_of(2 * m)
             for h in range(2):
                 n = 2 * m + h
-                tile, place = slot(n)
-                col = n - groups[i][0]
+                col = n - GROUPS[i][0]
                 nc.vector.scalar_tensor_tensor(
                     out=res[m][:, h, :],
-                    in0=tile[:, place, :],
+                    in0=y_of(n, n + 1)[:, 0, :],
                     scalar=inv[i][:, col : col + 1],
                     in1=gate[g][:, h, x, :],
                     op0=ALU.mult,
@@ -269,137 +233,114 @@ def tile_rows_a_relu2_gate_kernel(tc, qT, kT, t, v, og, out):
                 in_=res[m][:],
             )
 
-        load_t()
+        nc.scalar.dma_start(out=t_sb[:], in_=t.rearrange("(s r) o -> s (r o)", r=PACK))
         load_k(0)
-        load_q(q_first, 0, 0, P)
-        load_q(q_second, 0, P, 2 * P)
-        load_q(q_rest, 0, 2 * P, NQ)
-        load_k(1)
-        load_q(q_late[0], 1, 0, HALF)
+        load_q(0, 0)
+        load_q(0, 1)
         load_v(0)
-        load_q(q_late[1], 1, HALF, NQ)
-        load_og(0)
+        load_k(1)
+        load_q(1, 0)
+        load_q(1, 1)
         load_v(1)
+        load_og(0)
         load_og(1)
-        prep(0)
-        prep(1)
-        prep(2)
-        prep(3)
-        prep(4)
-        deal_k("s", 0, 0, 32)
-        prep(5)
-        prep(6)
-        prep(7)
-        prep(8)
-        deal_k("v", 0, 32, 128)
-        deal_q("s", 0, 0, 128)
-        prep(9)
-        deal_q("s", 0, 128, 256)
-        quant_k(0)
-        quant_q(0, 0, 128)
-        quant_q(0, 128, 256)
-        deal_q("v", 0, 256, 384)
+
+        nc.vector.memset(warm_in[:], 0.0)
+        nc.vector.scalar_tensor_tensor(out=t_abs[:], in0=t_sb[:], scalar=-1.0, in1=t_sb[:], op0=ALU.mult, op1=ALU.max)
+        nc.scalar.activation(out=half_root[:], in_=t_abs[:], func=ACT.Sqrt, scale=0.25)
+        nc.scalar.activation(out=warm_out[:], in_=warm_in[:], func=ACT.Sigmoid)
+        nc.vector.tensor_scalar_max(out=guarded[:], in0=half_root[:], scalar1=TINY)
+        nc.vector.reciprocal(out=recip[:], in_=guarded[:])
+        nc.vector.scalar_tensor_tensor(out=step[:], in0=recip[:], scalar=0.25, in1=t_abs[:], op0=ALU.mult, op1=ALU.mult)
+        nc.vector.tensor_tensor(out=t_root[:], in0=step[:], in1=half_root[:], op=ALU.add)
+        nc.vector.tensor_scalar(out=twice_pos[:], in0=t_sb[:], scalar1=0.0, scalar2=2.0, op0=ALU.is_ge, op1=ALU.mult)
+
+        pack_k(0)
+        pack_q(0, 0, 64, True)
+        pack_q(0, 64, 128, False)
+        pack_q(0, 128, 256, True)
+        quantize_k(0)
+        quantize_q(0, 0, 128)
         scores(0)
+        quantize_q(0, 128, 256)
         scores(1)
-        deal_q("s", 0, 384, 512)
-        rectify("v", 0)
-        rectify("s", 1)
-        quant_q(0, 256, 512)
-        square("v", 0)
-        rectify("v", 2)
+        pack_q(0, 256, 384, True)
+        pack_q(0, 384, 512, False)
+        quantize_q(0, 256, 512)
         scores(2)
-        square("s", 1)
-        square("v", 2)
+        pack_v(0)
+        rectify(0)
+        rectify(1)
         scores(3)
-        rectify("v", 3)
-        deal_k("v", 1, 0, 96)
-        rectify("s", 4)
-        square("v", 3)
-        rectify("v", 5)
-        rectify("v", 6)
-        deal_q("s", 1, 0, 128)
-        deal_q("v", 1, 128, 256)
-        deal_k("v", 1, 96, 128)
-        square("s", 4)
-        quant_q(1, 0, 256)
-        quant_k(1)
-        deal_v("v", 0, 0, 0, 128)
-        rectify("s", 7)
-        square("v", 5)
-        deal_v("v", 0, 1, 0, 64)
-        deal_q("v", 1, 256, 384)
-        deal_q("s", 1, 384, 512)
-        square("v", 6)
-        quant_w(0, 4)
-        deal_v("v", 0, 1, 64, 128)
+        square(0)
+        for n in range(2, 6):
+            rectify(n)
+            if n < 5:
+                square(n - 1)
+        pack_k(1)
+        quantize_w(0, 4)
+        quantize_v(0)
+        mix(0, 4)
+        pack_q(1, 0, 128, False)
+        pack_q(1, 128, 256, True)
+        quantize_k(1)
+        quantize_q(1, 0, 256)
         scores(4)
+        pack_v(1)
+        square(4)
+        pack_q(1, 256, 512, True)
+        rectify(6)
+        rectify(7)
         scores(5)
-        quant_q(1, 256, 512)
-        square("s", 7)
-        rectify("v", 8)
-        quant_v(0)
-        scores(6)
-        rectify("v", 9)
-        mix(0)
-        rectify("v", 10)
-        rectify("s", 11)
-        sigmoid(0, 0)
-        mix(1)
-        mix(2)
-        quant_w(4, 8)
-        mix(3)
-        denom(0)
-        deal_v("v", 1, 0, 0, 64)
+        denominator(0)
+        rectify(8)
         invert(0)
-        mix(4)
-        square("v", 8)
-        deal_v("v", 1, 0, 64, 128)
-        square("v", 9)
-        quant_w(8, 10)
-        mix(5)
-        rectify("s", 12)
-        deal_v("v", 1, 1, 0, 128)
-        mix(6)
-        sigmoid(0, 1)
+        for n in range(9, 12):
+            rectify(n)
+        for n in range(5, 10):
+            square(n)
+        quantize_q(1, 256, 512)
+        scores(6)
+        quantize_w(4, 8)
+        mix(4, 8)
         scores(7)
+        quantize_v(1)
+        sigmoid(0, 0)
+        sigmoid(0, 1)
+        square(10)
+        square(11)
         finish(0)
-        square("v", 10)
-        rectify("v", 13)
-        mix(7)
-        denom(1)
-        quant_v(1)
         finish(1)
-        square("s", 11)
-        square("s", 12)
-        mix(8)
-        square("v", 13)
-        quant_w(10, 12)
-        mix(9)
+        rectify(12)
+        denominator(1)
+        quantize_w(8, 10)
         invert(1)
+        quantize_w(10, 12)
+        mix(8, 12)
         sigmoid(1, 0)
-        rectify("v", 14)
-        mix(10)
-        mix(11)
+        rectify(13)
+        square(12)
+        square(13)
         finish(2)
-        rectify("s", 15)
-        denom(2)
-        square("v", 14)
+        rectify(14)
         finish(3)
-        square("s", 15)
+        denominator(2)
+        rectify(15)
+        square(14)
+        square(15)
         sigmoid(1, 1)
         invert(2)
-        quant_w(12, 14)
+        quantize_w(12, 14)
+        mix(12, 14)
         finish(4)
         finish(5)
-        quant_w(14, 15)
-        mix(12)
-        mix(13)
-        denom(3)
-        quant_w(15, 16)
-        mix(14)
+        quantize_w(14, 15)
+        mix(14, 15)
+        quantize_w(15, 16)
+        mix(15, 16)
+        denominator(3)
         invert(3)
-        mix(15)
+        denominator(4)
         finish(6)
-        denom(4)
         invert(4)
         finish(7)

@@ -60,7 +60,6 @@ def tile_rows_a_relu2_gate_kernel(tc, qT, kT, t, v, og, out):
         res = tiles("res", UNITS // 2, [P, 2, E], F32)
         t_sb, t_abs, half_root, guarded, recip, step, t_root, twice_pos = tiles("t_work", 8, [P, PACK], F32)
         t_sign = tiles("t_sign", PAIRS, [P, PACK], F32)
-        warm_in, warm_out = tiles("warm", 2, [P, 1], F32)
         score = [ps.tile([P, PACK, P], F32, name="score" + str(i)) for i in range(2 * SCORE_BANKS)]
         y_bank = [ps.tile([P, 4, E], F32, name="y_bank" + str(i)) for i in range(2)]
 
@@ -79,10 +78,10 @@ def tile_rows_a_relu2_gate_kernel(tc, qT, kT, t, v, og, out):
                 in_=v[2 * g : 2 * g + 2].rearrange("h (s r) e -> s h (r e)", r=PACK),
             )
 
-        def load_og(g):
-            nc.sync.dma_start(
-                out=og_raw[g][:].rearrange("p h x e -> p (h x) e"),
-                in_=og[2 * g : 2 * g + 2].rearrange("h (x p) e -> p (h x) e", p=P),
+        def load_og(queue, g, i0, i1):
+            queue.dma_start(
+                out=og_raw[g][:].rearrange("p h x e -> p (h x) e")[:, i0:i1, :],
+                in_=og[2 * g : 2 * g + 2].rearrange("h (x p) e -> p (h x) e", p=P)[:, i0:i1, :],
             )
 
         def copy(on_scalar, dst, src):
@@ -202,9 +201,8 @@ def tile_rows_a_relu2_gate_kernel(tc, qT, kT, t, v, og, out):
                     stop=True,
                 )
 
-        def sigmoid(g, c):
-            tiles_c = slice(2 * c, 2 * c + 2)
-            nc.scalar.activation(out=gate[g][:, :, tiles_c, :], in_=og_raw[g][:, :, tiles_c, :], func=ACT.Sigmoid)
+        def sigmoid(g, h0, h1, x0, x1):
+            nc.scalar.activation(out=gate[g][:, h0:h1, x0:x1, :], in_=og_raw[g][:, h0:h1, x0:x1, :], func=ACT.Sigmoid)
 
         def denominator(i):
             n0, n1 = GROUPS[i]
@@ -228,12 +226,10 @@ def tile_rows_a_relu2_gate_kernel(tc, qT, kT, t, v, og, out):
                     op0=ALU.mult,
                     op1=ALU.mult,
                 )
-            nc.sync.dma_start(
-                out=out[2 * g : 2 * g + 2, x * P : (x + 1) * P, :].rearrange("h p e -> p h e"),
-                in_=res[m][:],
-            )
+                nc.sync.dma_start(out=out[2 * g + h, x * P : (x + 1) * P, :], in_=res[m][:, h, :])
 
         nc.scalar.dma_start(out=t_sb[:], in_=t.rearrange("(s r) o -> s (r o)", r=PACK))
+        load_og(nc.scalar, 0, 0, 1)
         load_k(0)
         load_q(0, 0)
         load_q(0, 1)
@@ -242,53 +238,56 @@ def tile_rows_a_relu2_gate_kernel(tc, qT, kT, t, v, og, out):
         load_q(1, 0)
         load_q(1, 1)
         load_v(1)
-        load_og(0)
-        load_og(1)
+        load_og(nc.sync, 0, 1, 2 * TILES)
+        load_og(nc.sync, 1, 0, 2 * TILES)
 
-        nc.vector.memset(warm_in[:], 0.0)
         nc.vector.scalar_tensor_tensor(out=t_abs[:], in0=t_sb[:], scalar=-1.0, in1=t_sb[:], op0=ALU.mult, op1=ALU.max)
         nc.scalar.activation(out=half_root[:], in_=t_abs[:], func=ACT.Sqrt, scale=0.25)
-        nc.scalar.activation(out=warm_out[:], in_=warm_in[:], func=ACT.Sigmoid)
+        sigmoid(0, 0, 1, 0, 1)
         nc.vector.tensor_scalar_max(out=guarded[:], in0=half_root[:], scalar1=TINY)
         nc.vector.reciprocal(out=recip[:], in_=guarded[:])
         nc.vector.scalar_tensor_tensor(out=step[:], in0=recip[:], scalar=0.25, in1=t_abs[:], op0=ALU.mult, op1=ALU.mult)
         nc.vector.tensor_tensor(out=t_root[:], in0=step[:], in1=half_root[:], op=ALU.add)
         nc.vector.tensor_scalar(out=twice_pos[:], in0=t_sb[:], scalar1=0.0, scalar2=2.0, op0=ALU.is_ge, op1=ALU.mult)
 
+
         pack_k(0)
-        pack_q(0, 0, 64, True)
-        pack_q(0, 64, 128, False)
-        pack_q(0, 128, 256, True)
         quantize_k(0)
-        quantize_q(0, 0, 128)
+        pack_q(0, 0, P // 2, True)
+        pack_q(0, P // 2, P, False)
+        pack_q(0, P, 2 * P, True)
+        quantize_q(0, 0, P)
         scores(0)
-        quantize_q(0, 128, 256)
+        quantize_q(0, P, HALF)
         scores(1)
-        pack_q(0, 256, 384, True)
-        pack_q(0, 384, 512, False)
-        quantize_q(0, 256, 512)
+        pack_q(0, HALF, 3 * P, True)
+        pack_q(0, 3 * P, NQ, False)
+        quantize_q(0, HALF, NQ)
         scores(2)
+
         pack_v(0)
         rectify(0)
         rectify(1)
         scores(3)
         square(0)
-        for n in range(2, 6):
+        for n in range(2, 5):
             rectify(n)
-            if n < 5:
-                square(n - 1)
+            square(n - 1)
+        rectify(5)
+
         pack_k(1)
         quantize_w(0, 4)
         quantize_v(0)
         mix(0, 4)
-        pack_q(1, 0, 128, False)
-        pack_q(1, 128, 256, True)
+        pack_q(1, 0, P, False)
+        pack_q(1, P, HALF, True)
         quantize_k(1)
-        quantize_q(1, 0, 256)
+        quantize_q(1, 0, HALF)
         scores(4)
+
         pack_v(1)
         square(4)
-        pack_q(1, 256, 512, True)
+        pack_q(1, HALF, NQ, True)
         rectify(6)
         rectify(7)
         scores(5)
@@ -299,14 +298,15 @@ def tile_rows_a_relu2_gate_kernel(tc, qT, kT, t, v, og, out):
             rectify(n)
         for n in range(5, 10):
             square(n)
-        quantize_q(1, 256, 512)
+
+        quantize_q(1, HALF, NQ)
         scores(6)
         quantize_w(4, 8)
         mix(4, 8)
         scores(7)
         quantize_v(1)
-        sigmoid(0, 0)
-        sigmoid(0, 1)
+        sigmoid(0, 0, 1, 1, TILES)
+        sigmoid(0, 1, 2, 0, TILES)
         square(10)
         square(11)
         finish(0)
@@ -317,7 +317,7 @@ def tile_rows_a_relu2_gate_kernel(tc, qT, kT, t, v, og, out):
         invert(1)
         quantize_w(10, 12)
         mix(8, 12)
-        sigmoid(1, 0)
+        sigmoid(1, 0, 2, 0, 2)
         rectify(13)
         square(12)
         square(13)
@@ -328,8 +328,9 @@ def tile_rows_a_relu2_gate_kernel(tc, qT, kT, t, v, og, out):
         rectify(15)
         square(14)
         square(15)
-        sigmoid(1, 1)
+        sigmoid(1, 0, 2, 2, TILES)
         invert(2)
+
         quantize_w(12, 14)
         mix(12, 14)
         finish(4)

from contextlib import ExitStack

import concourse.mybir as mybir

H, D, NQ, N, E = 4, 256, 512, 512, 128
FLOPS = 2 * H * N * NQ * D + 2 * H * NQ * N * E

F32 = mybir.dt.float32
BF16 = mybir.dt.bfloat16
U32 = mybir.dt.uint32
U8 = mybir.dt.uint8
FP8X4 = mybir.dt.float8_e4m3fn_x4
ACT = mybir.ActivationFunctionType
ALU = mybir.AluOpType

P = 128
PACK = 4
ROWS = 64
PAIRS = 2
TILES = NQ // P
HALF = NQ // 2
UNITS = H * TILES
SCORE_BANKS = 3
GROUPS = [(0, 4), (4, 8), (8, 12), (12, 14), (14, 16)]
ON_SCALAR = (1, 13)
KEY_SPLIT = (80, 48)
TINY = 1e-30


def tile_rows_a_relu2_gate_kernel(tc, qT, kT, t, v, og, out):
    nc = tc.nc
    with ExitStack() as ctx:
        sb = ctx.enter_context(tc.tile_pool(name="sb", bufs=1))
        ps = ctx.enter_context(tc.psum_pool(name="ps", bufs=1))
        ctx.enter_context(tc.manual_schedule())

        def tiles(name, count, shape, dtype):
            return [sb.tile(shape, dtype, name=name + str(i), align_bytes=64) for i in range(count)]

        k_raw = tiles("k_raw", PAIRS, [P, PACK, N], F32)
        q_raw = tiles("q_raw", 2 * PAIRS, [P, PACK, HALF], F32)
        v_raw = tiles("v_raw", PAIRS, [P, 2, PACK, E], F32)
        og_raw = tiles("og_raw", PAIRS, [P, 2, TILES, E], F32)
        gate = tiles("gate", PAIRS, [P, 2, TILES, E], F32)
        k_bf = tiles("k_bf", PAIRS, [P, PACK, P, PACK], BF16)
        q_bf = tiles("q_bf", PAIRS, [P, NQ, PACK], BF16)
        v_bf = tiles("v_bf", PAIRS, [P, 2, E, PACK], BF16)
        k_codes = tiles("k_codes", PAIRS, [P, N], U32)
        k_scales = tiles("k_scales", PAIRS, [P, N], U8)
        q_codes = tiles("q_codes", PAIRS, [P, NQ], U32)
        q_scales = tiles("q_scales", PAIRS, [P, NQ], U8)
        v_codes = tiles("v_codes", PAIRS, [P, 2 * E], U32)
        v_scales = tiles("v_scales", PAIRS, [P, 2 * E], U8)
        root_w = tiles("root_w", UNITS, [P, PACK * P], F32)
        w_bf = sb.tile([P, UNITS, P, PACK], BF16, name="w_bf", align_bytes=64)
        w_codes = sb.tile([P, UNITS, P], U32, name="w_codes", align_bytes=64)
        w_scales = sb.tile([P, UNITS, P], U8, name="w_scales", align_bytes=64)
        den = tiles("den", len(GROUPS), [P, 4], F32)
        inv = tiles("inv", len(GROUPS), [P, 4], F32)
        res = tiles("res", UNITS // 2, [P, 2, E], F32)
        t_sb, t_abs, half_root, guarded, recip, step, t_root, twice_pos = tiles("t_work", 8, [P, PACK], F32)
        t_sign = tiles("t_sign", PAIRS, [P, PACK], F32)
        score = [ps.tile([P, PACK, P], F32, name="score" + str(i)) for i in range(2 * SCORE_BANKS)]
        y_bank = [ps.tile([P, 4, E], F32, name="y_bank" + str(i)) for i in range(2)]

        def feature_rows(x, g):
            return x[2 * g : 2 * g + 2].rearrange("h (p j) n -> (h p) j n", j=PACK)

        def load_k(g):
            nc.sync.dma_start(out=k_raw[g][:], in_=feature_rows(kT, g))

        def load_q(g, c):
            nc.sync.dma_start(out=q_raw[2 * g + c][:], in_=feature_rows(qT, g)[:, :, c * HALF : (c + 1) * HALF])

        def load_v(g):
            nc.sync.dma_start(
                out=v_raw[g][:].rearrange("s h r e -> s h (r e)"),
                in_=v[2 * g : 2 * g + 2].rearrange("h (s r) e -> s h (r e)", r=PACK),
            )

        def load_og(queue, g, i0, i1):
            queue.dma_start(
                out=og_raw[g][:].rearrange("p h x e -> p (h x) e")[:, i0:i1, :],
                in_=og[2 * g : 2 * g + 2].rearrange("h (x p) e -> p (h x) e", p=P)[:, i0:i1, :],
            )

        def copy(on_scalar, dst, src):
            if on_scalar:
                nc.scalar.copy(out=dst, in_=src)
            else:
                nc.vector.tensor_copy(out=dst, in_=src)

        def pack_k(g):
            dst = k_bf[g][:].rearrange("p r s j -> p s j r")
            src = k_raw[g][:].rearrange("p j (s r) -> p s j r", r=PACK)
            copy(False, dst[:, : KEY_SPLIT[g]], src[:, : KEY_SPLIT[g]])
            copy(True, dst[:, KEY_SPLIT[g] :], src[:, KEY_SPLIT[g] :])

        def pack_q(g, c0, c1, on_scalar):
            src = q_raw[2 * g + c0 // HALF][:, :, c0 % HALF : c0 % HALF + c1 - c0]
            copy(
                on_scalar,
                q_bf[g][:, c0:c1, :].rearrange("p (c i) j -> p c j i", i=2),
                src.rearrange("p j (c i) -> p c j i", i=2),
            )

        def pack_v(g):
            nc.vector.tensor_scalar_add(out=t_sign[g][:], in0=twice_pos[:], scalar1=-1.0)
            for h in range(2):
                nc.gpsimd.tensor_tensor(
                    out=v_bf[g][:, h],
                    in0=v_raw[g][:, h].rearrange("s r e -> s e r"),
                    in1=t_sign[g][:].unsqueeze(1).to_broadcast([P, E, PACK]),
                    op=ALU.mult,
                )

        def quantize(codes, scales, src):
            nc.vector.quantize_mx(out=codes.bitcast(FP8X4), scales=scales, in_=src)

        def quantize_k(g):
            quantize(k_codes[g][:], k_scales[g][:], k_bf[g][:].rearrange("p r s j -> p (r s j)"))

        def quantize_q(g, c0, c1):
            quantize(q_codes[g][:, c0:c1], q_scales[g][:, c0:c1], q_bf[g][:, c0:c1, :].rearrange("p n j -> p (n j)"))

        def quantize_v(g):
            quantize(v_codes[g][:], v_scales[g][:], v_bf[g][:].rearrange("s h e r -> s (h e r)"))

        def quantize_w(n0, n1):
            quantize(
                w_codes[:, n0:n1, :].rearrange("s n q -> s (n q)"),
                w_scales[:, n0:n1, :].rearrange("s n q -> s (n q)"),
                w_bf[:, n0:n1].rearrange("s n q r -> s (n q r)"),
            )

        def score_bank(n):
            return score[(n % 2) * SCORE_BANKS + (n // 2) % SCORE_BANKS]

        def scores(m):
            g, x = divmod(m, TILES)
            queries = slice(x * P, (x + 1) * P)
            for r in range(PACK):
                keys = slice(r * P, (r + 1) * P)
                for h in range(2):
                    rows = slice(h * ROWS, (h + 1) * ROWS)
                    nc.tensor.matmul_mx(
                        out=score_bank(2 * m + h)[:, r, :],
                        lhsT=k_codes[g][rows, keys].bitcast(FP8X4),
                        lhsT_scale=k_scales[g][rows, keys],
                        rhs=q_codes[g][rows, queries].bitcast(FP8X4),
                        rhs_scale=q_scales[g][rows, queries],
                        start=True,
                        stop=True,
                    )

        def rectify(n):
            if n in ON_SCALAR:
                for r in range(PACK):
                    nc.scalar.activation(
                        out=root_w[n][:, r * P : (r + 1) * P],
                        in_=score_bank(n)[:, r, :],
                        func=ACT.Relu,
                        scale=t_root[:, r : r + 1],
                    )
            else:
                nc.vector.scalar_tensor_tensor(
                    out=root_w[n][:].rearrange("s (q r) -> s q r", r=PACK),
                    in0=score_bank(n)[:].rearrange("s r q -> s q r"),
                    scalar=0.0,
                    in1=t_root[:].unsqueeze(1).to_broadcast([P, P, PACK]),
                    op0=ALU.max,
                    op1=ALU.mult,
                )

        def square(n):
            if n in ON_SCALAR:
                dst = w_bf[:, n].rearrange("s (c i) r -> s c r i", i=2)
                src = root_w[n][:].rearrange("s (r c i) -> s c r i", r=PACK, i=2)
            else:
                dst = w_bf[:, n].rearrange("s q r -> s (q r)")
                src = root_w[n][:]
            nc.scalar.activation(out=dst, in_=src, func=ACT.Square)

        def group_of(n):
            return [i for i, (n0, n1) in enumerate(GROUPS) if n0 <= n < n1][0]

        def y_of(n0, n1):
            i = group_of(n0)
            return y_bank[i % 2][:, n0 - GROUPS[i][0] : n1 - GROUPS[i][0], :]

        def mix(n0, n1):
            for n in range(n0, n1):
                cols = slice((n % 2) * E, (n % 2 + 1) * E)
                nc.tensor.matmul_mx(
                    out=y_of(n, n + 1)[:, 0, :],
                    lhsT=w_codes[:, n, :].bitcast(FP8X4),
                    lhsT_scale=w_scales[:, n, :],
                    rhs=v_codes[n // 8][:, cols].bitcast(FP8X4),
                    rhs_scale=v_scales[n // 8][:, cols],
                    start=True,
                    stop=True,
                )

        def sigmoid(g, h0, h1, x0, x1):
            nc.scalar.activation(out=gate[g][:, h0:h1, x0:x1, :], in_=og_raw[g][:, h0:h1, x0:x1, :], func=ACT.Sigmoid)

        def denominator(i):
            n0, n1 = GROUPS[i]
            nc.vector.tensor_scalar_add(out=den[i][:, : n1 - n0], in0=y_of(n0, n1)[:, :, E - 1], scalar1=1.0)

        def invert(i):
            n0, n1 = GROUPS[i]
            nc.vector.reciprocal(out=inv[i][:, : n1 - n0], in_=den[i][:, : n1 - n0])

        def finish(m):
            g, x = divmod(m, TILES)
            i = group_of(2 * m)
            for h in range(2):
                n = 2 * m + h
                col = n - GROUPS[i][0]
                nc.vector.scalar_tensor_tensor(
                    out=res[m][:, h, :],
                    in0=y_of(n, n + 1)[:, 0, :],
                    scalar=inv[i][:, col : col + 1],
                    in1=gate[g][:, h, x, :],
                    op0=ALU.mult,
                    op1=ALU.mult,
                )
                nc.sync.dma_start(out=out[2 * g + h, x * P : (x + 1) * P, :], in_=res[m][:, h, :])

        nc.scalar.dma_start(out=t_sb[:], in_=t.rearrange("(s r) o -> s (r o)", r=PACK))
        load_og(nc.scalar, 0, 0, 1)
        load_k(0)
        load_q(0, 0)
        load_q(0, 1)
        load_v(0)
        load_k(1)
        load_q(1, 0)
        load_q(1, 1)
        load_v(1)
        load_og(nc.sync, 0, 1, 2 * TILES)
        load_og(nc.sync, 1, 0, 2 * TILES)

        nc.vector.scalar_tensor_tensor(out=t_abs[:], in0=t_sb[:], scalar=-1.0, in1=t_sb[:], op0=ALU.mult, op1=ALU.max)
        nc.scalar.activation(out=half_root[:], in_=t_abs[:], func=ACT.Sqrt, scale=0.25)
        sigmoid(0, 0, 1, 0, 1)
        nc.vector.tensor_scalar_max(out=guarded[:], in0=half_root[:], scalar1=TINY)
        nc.vector.reciprocal(out=recip[:], in_=guarded[:])
        nc.vector.scalar_tensor_tensor(out=step[:], in0=recip[:], scalar=0.25, in1=t_abs[:], op0=ALU.mult, op1=ALU.mult)
        nc.vector.tensor_tensor(out=t_root[:], in0=step[:], in1=half_root[:], op=ALU.add)
        nc.vector.tensor_scalar(out=twice_pos[:], in0=t_sb[:], scalar1=0.0, scalar2=2.0, op0=ALU.is_ge, op1=ALU.mult)


        pack_k(0)
        quantize_k(0)
        pack_q(0, 0, P // 2, True)
        pack_q(0, P // 2, P, False)
        pack_q(0, P, 2 * P, True)
        quantize_q(0, 0, P)
        scores(0)
        quantize_q(0, P, HALF)
        scores(1)
        pack_q(0, HALF, 3 * P, True)
        pack_q(0, 3 * P, NQ, False)
        quantize_q(0, HALF, NQ)
        scores(2)

        pack_v(0)
        rectify(0)
        rectify(1)
        scores(3)
        square(0)
        for n in range(2, 5):
            rectify(n)
            square(n - 1)
        rectify(5)

        pack_k(1)
        quantize_w(0, 4)
        quantize_v(0)
        mix(0, 4)
        pack_q(1, 0, P, False)
        pack_q(1, P, HALF, True)
        quantize_k(1)
        quantize_q(1, 0, HALF)
        scores(4)

        pack_v(1)
        square(4)
        pack_q(1, HALF, NQ, True)
        rectify(6)
        rectify(7)
        scores(5)
        denominator(0)
        rectify(8)
        invert(0)
        for n in range(9, 12):
            rectify(n)
        for n in range(5, 10):
            square(n)

        quantize_q(1, HALF, NQ)
        scores(6)
        quantize_w(4, 8)
        mix(4, 8)
        scores(7)
        quantize_v(1)
        sigmoid(0, 0, 1, 1, TILES)
        sigmoid(0, 1, 2, 0, TILES)
        square(10)
        square(11)
        finish(0)
        finish(1)
        rectify(12)
        denominator(1)
        quantize_w(8, 10)
        invert(1)
        quantize_w(10, 12)
        mix(8, 12)
        sigmoid(1, 0, 2, 0, 2)
        rectify(13)
        square(12)
        square(13)
        finish(2)
        rectify(14)
        finish(3)
        denominator(2)
        rectify(15)
        square(14)
        square(15)
        sigmoid(1, 0, 2, 2, TILES)
        invert(2)

        quantize_w(12, 14)
        mix(12, 14)
        finish(4)
        finish(5)
        quantize_w(14, 15)
        mix(14, 15)
        quantize_w(15, 16)
        mix(15, 16)
        denominator(3)
        invert(3)
        denominator(4)
        finish(6)
        invert(4)
        finish(7)
